import numpy as np
import ml_dtypes


def mxq(x, axis, fmt="e4m3"):
    dtype, down = {"e4m3": (ml_dtypes.float8_e4m3fn, 7), "e5m2": (ml_dtypes.float8_e5m2, 14)}[fmt]
    v = np.moveaxis(np.asarray(x, np.float32).astype(ml_dtypes.bfloat16).astype(np.float64), axis, -1)
    blocks = v.reshape(v.shape[:-1] + (-1, 32))
    amax = np.abs(blocks).max(-1, keepdims=True)
    byte = np.maximum(np.where(amax > 0, np.frexp(amax)[1] - 1 + 127, 0) - down, 1)
    scale = np.exp2(byte - 127.0)
    codes = (blocks / scale).astype(np.float32).astype(dtype).astype(np.float64)
    return np.moveaxis((codes * scale).reshape(v.shape), -1, axis)


WIDE = False


def mx_kscale(k):
    if not WIDE:
        return np.ones(k)
    levels = np.array([10, -10, 5, -5, 0])
    if k % 512:
        return np.exp2(np.random.permutation(np.resize(levels, k // 32))).repeat(32)
    a = np.empty((k // 512, 16))
    for p in range(k // 512):
        a[p, :8] = np.random.permutation(np.resize(levels, 8))
        for g in range(8):
            far = levels[np.abs(levels - a[p, g]) >= 10]
            a[p, g + 8] = far[np.random.randint(len(far))]
    return np.exp2(a.ravel()).repeat(32)


def f64(x):
    return np.asarray(x).astype(np.float64)


def striped(idx):
    return np.tile(idx.reshape(-1, 16).T, (8, 1)).astype(np.uint16)


def unstriped(offs):
    return offs[:16].T.reshape(-1).astype(np.int64)


def pack_weight(w):
    k, n = w.shape
    w = f64(np.asarray(w, np.float32).astype(ml_dtypes.bfloat16)).reshape(k // 32, 32, n)
    amax = np.abs(w).max(1)
    byte = np.clip(np.where(amax > 0, np.frexp(amax)[1] - 1 + 127 - 7, 1), 1, 254)
    scaled = (w * np.exp2(127.0 - byte)[:, None, :]).reshape(k, n).astype(np.float32)
    words = np.ascontiguousarray(scaled.reshape(k // 512, 128, 4, n).transpose(0, 1, 3, 2)).astype(ml_dtypes.float8_e4m3fn).view(np.uint8)
    return words, np.ascontiguousarray(byte.astype(np.uint8).reshape(k // 512, 16, n))


def unpack_weight(words, scales):
    g, p, n, _ = words.shape
    vals = np.ascontiguousarray(words).view(ml_dtypes.float8_e4m3fn).astype(np.float64) * np.repeat(np.exp2(scales.astype(np.float64) - 127.0), 8, axis=1)[..., None]
    return vals.transpose(0, 1, 3, 2).reshape(g * 512, n)


K, T, S, V = 1024, 1024, 512, 256


def setup_inputs():
    n = np.random.standard_normal
    s = mx_kscale(K)[:, None]
    packed_xT = pack_weight(n((K, T)) * s)
    return {
        "x_words": packed_xT[0],
        "x_scales": packed_xT[1],
        "hT": (n((K, V)) / np.sqrt(K) / s).astype(np.float32),
        "g1": ((np.random.uniform(size=(V, S)) < 0.5) * 1.0).astype(np.float32),
        "g2": ((np.random.uniform(size=(V, S)) < 0.5) * 1.0).astype(np.float32),
        "offs": striped(np.random.permutation(T)[:S]),
    }


def reference(x_words, x_scales, hT, g1, g2, offs):
    hTq = mxq(f64(hT), 0, "e4m3")
    xq = unpack_weight(x_words, x_scales)[:, unstriped(offs)]
    y = hTq.T @ xq
    ex = np.exp(y - y.max(axis=1, keepdims=True))
    p0 = ex / ex.sum(axis=1, keepdims=True)
    r1 = p0 * f64(g1)
    t1 = r1.sum(axis=1, keepdims=True)
    p1 = p0 + r1 - (p0 * t1)
    r2 = p1 * f64(g2)
    t2 = r2.sum(axis=1, keepdims=True)
    p2 = p1 + r2 - (p1 * t2)
    return np.log(512.0 * p2 + 0.01)

@@ -1,0 +1,154 @@
+from contextlib import ExitStack
+
+import concourse.mybir as mybir
+
+K, T, S, V = 1024, 1024, 512, 256
+FLOPS = 2 * K * S * V
+
+F32 = mybir.dt.float32
+BF16 = mybir.dt.bfloat16
+I32 = mybir.dt.int32
+U32 = mybir.dt.uint32
+U16 = mybir.dt.uint16
+U8 = mybir.dt.uint8
+FP8X4 = mybir.dt.float8_e4m3fn_x4
+ALU = mybir.AluOpType
+ACT = mybir.ActivationFunctionType
+AX = mybir.AxisListType
+
+P = 128
+PACK = 4
+K_PASS = P * PACK
+PASSES = K // K_PASS
+BLOCKS = V // P
+QUADS = 4
+QUAD = P // QUADS
+
+
+def tile_picked_ysynth_two_p_kernel(tc, x_words, x_scales, hT, g1, g2, offs, out):
+    nc = tc.nc
+    with ExitStack() as ctx:
+        keep = ctx.enter_context(tc.tile_pool(name="keep", bufs=1))
+        psum = ctx.enter_context(tc.psum_pool(name="psum", bufs=1))
+
+        offsets = keep.tile([P, S // 16], U16, name="offsets")
+        nc.sync.dma_start(offsets[:], offs)
+
+        scale_table = keep.tile([P, T], U8, name="scale_table", align_bytes=64)
+        nc.gpsimd.memset(scale_table[:].bitcast(I32), 0)
+        for q in range(QUADS):
+            nc.scalar.dma_start(
+                scale_table[:].bitcast(I32)[QUAD * q : QUAD * q + 4 * PASSES, :],
+                x_scales[:, 4 * q : 4 * q + 4, :].bitcast(I32),
+            )
+
+        word_table = [keep.tile([P, T], I32, name=f"word_table{o}", align_bytes=64) for o in range(PASSES)]
+        h_raw = [[keep.tile([P, PACK, P], F32, name=f"h_raw{b}_{o}") for o in range(PASSES)] for b in range(BLOCKS)]
+        g1_sb = [keep.tile([P, S], F32, name=f"g1_sb{b}") for b in range(BLOCKS)]
+        g2_sb = [keep.tile([P, S], F32, name=f"g2_sb{b}") for b in range(BLOCKS)]
+
+        for o in range(PASSES):
+            nc.sync.dma_start(word_table[o][:], x_words[o].rearrange("p n t -> p (n t)").bitcast(I32))
+        for b in range(BLOCKS):
+            for o in range(PASSES):
+                rows = hT[o * K_PASS : (o + 1) * K_PASS, b * P : (b + 1) * P]
+                nc.sync.dma_start(h_raw[b][o][:], rows.rearrange("(p j) m -> p j m", j=PACK))
+        for g, g_sb in ((g1, g1_sb), (g2, g2_sb)):
+            for b in range(BLOCKS):
+                nc.sync.dma_start(g_sb[b][:], g[b * P : (b + 1) * P, :])
+
+        x_scale = keep.tile([P, S], U8, name="x_scale", align_bytes=64)
+        nc.vector.tensor_copy(x_scale[:], scale_table[:].indirect(offsets[:]))
+        x_codes = [keep.tile([P, S], U32, name=f"x_codes{o}", align_bytes=64) for o in range(PASSES)]
+        for o in range(PASSES):
+            nc.vector.tensor_copy(x_codes[o][:], word_table[o][:].bitcast(U32).indirect(offsets[:]))
+
+        h_codes = [keep.tile([P, PASSES * P], U32, name=f"h_codes{b}", align_bytes=64) for b in range(BLOCKS)]
+        h_scale = [keep.tile([P, PASSES * P], U8, name=f"h_scale{b}", align_bytes=64) for b in range(BLOCKS)]
+        grouped = [keep.tile([P, PASSES, P, PACK], BF16, name=f"grouped{b}", align_bytes=64) for b in range(BLOCKS)]
+        logits = [psum.tile([P, S], F32, name=f"logits{b}") for b in range(BLOCKS)]
+
+        def cast_h(b, o):
+            nc.scalar.activation(
+                grouped[b][:, o].rearrange("p (c i) j -> p c j i", i=4),
+                h_raw[b][o][:].rearrange("p j (c i) -> p c j i", i=4),
+                ACT.Copy,
+            )
+
+        def quantize_h(b, o0, o1):
+            nc.vector.quantize_mx(
+                out=h_codes[b][:, o0 * P : o1 * P].bitcast(FP8X4),
+                scales=h_scale[b][:, o0 * P : o1 * P],
+                in_=grouped[b][:, o0:o1].rearrange("p o m j -> p (o m j)"),
+            )
+
+        def product(b, o):
+            nc.tensor.matmul_mx(
+                out=logits[b][:],
+                lhsT=h_codes[b][:, o * P : (o + 1) * P].bitcast(FP8X4),
+                lhsT_scale=h_scale[b][:, o * P : (o + 1) * P],
+                rhs=x_codes[o][:].bitcast(FP8X4),
+                rhs_scale=x_scale[4 * o :, :],
+                start=(o == 0),
+                stop=(o == PASSES - 1),
+            )
+
+        def column(name, width=1):
+            return [keep.tile([P, width], F32, name=f"{name}{b}") for b in range(BLOCKS)]
+
+        neg_max, total, inv_total = column("neg_max"), column("total"), column("inv_total")
+        raw1, norm1, raw2, norm2 = column("raw1_", 2), column("norm1_", 2), column("raw2_"), column("norm2_")
+        e, u, v, res = column("e", S), column("u", S), column("v", S), column("res", S)
+
+        def softmax(b):
+            nc.vector.reduce_max(neg_max[b][:], logits[b][:], AX.X, negate=True)
+            nc.scalar.activation(e[b][:], logits[b][:], ACT.Exp, bias=neg_max[b][:], accum_out=total[b][:])
+
+        def mass1(b):
+            nc.vector.scalar_tensor_tensor(u[b][:], g1_sb[b][:], -1.0, e[b][:], ALU.add, ALU.mult, accum_out=raw1[b][:, 0:1])
+            nc.vector.reciprocal(inv_total[b][:], total[b][:])
+
+        def small1(b):
+            nc.vector.tensor_scalar(norm1[b][:], raw1[b][:], inv_total[b][:], None, ALU.mult)
+
+        def round1(b):
+            nc.vector.scalar_tensor_tensor(u[b][:], g1_sb[b][:], norm1[b][:, 0:1], e[b][:], ALU.subtract, ALU.mult)
+
+        def mass2(b):
+            nc.vector.scalar_tensor_tensor(v[b][:], g2_sb[b][:], -1.0, u[b][:], ALU.add, ALU.mult, accum_out=raw2[b][:])
+
+        def small2(b):
+            nc.vector.tensor_scalar(norm2[b][:], raw2[b][:], inv_total[b][:], None, ALU.mult)
+
+        def round2(b, c0, c1):
+            nc.vector.scalar_tensor_tensor(v[b][:, c0:c1], g2_sb[b][:, c0:c1], norm2[b][:], u[b][:, c0:c1], ALU.subtract, ALU.mult)
+            nc.scalar.activation(res[b][:, c0:c1], v[b][:, c0:c1], ACT.Ln, bias=0.01, scale=norm1[b][:, 1:2])
+            nc.sync.dma_start(out[b * P : (b + 1) * P, c0:c1], res[b][:, c0:c1])
+
+        for b in range(BLOCKS):
+            nc.vector.memset(raw1[b][:, 1:2], float(S))
+
+        for o in range(PASSES):
+            cast_h(0, o)
+            quantize_h(0, o, o + 1)
+            product(0, o)
+        for o in range(PASSES):
+            cast_h(1, o)
+        quantize_h(1, 0, PASSES)
+        for o in range(PASSES):
+            product(1, o)
+        softmax(0)
+        mass1(0)
+        softmax(1)
+        small1(0)
+        round1(0)
+        mass1(1)
+        mass2(0)
+        small1(1)
+        round1(1)
+        small2(0)
+        round2(0, 0, S)
+        mass2(1)
+        small2(1)
+        round2(1, 0, S // 2)
+        round2(1, S // 2, S)

@@ -34,121 +34,107 @@ def tile_picked_ysynth_two_p_kernel(tc, x_words, x_scales, hT, g1, g2, offs, out
         offsets = keep.tile([P, S // 16], U16, name="offsets")
         nc.sync.dma_start(offsets[:], offs)
 
-        scale_table = keep.tile([P, T], U8, name="scale_table", align_bytes=64)
-        nc.gpsimd.memset(scale_table[:].bitcast(I32), 0)
-        for q in range(QUADS):
-            nc.scalar.dma_start(
-                scale_table[:].bitcast(I32)[QUAD * q : QUAD * q + 4 * PASSES, :],
-                x_scales[:, 4 * q : 4 * q + 4, :].bitcast(I32),
-            )
+        scale_table = keep.tile([P, T], U8, name="scale_table", tag="scale_slot", align_bytes=64)
+        nc.vector.memset(scale_table[:].bitcast(I32), 0)
 
         word_table = [keep.tile([P, T], I32, name=f"word_table{o}", align_bytes=64) for o in range(PASSES)]
         h_raw = [[keep.tile([P, PACK, P], F32, name=f"h_raw{b}_{o}") for o in range(PASSES)] for b in range(BLOCKS)]
         g1_sb = [keep.tile([P, S], F32, name=f"g1_sb{b}") for b in range(BLOCKS)]
         g2_sb = [keep.tile([P, S], F32, name=f"g2_sb{b}") for b in range(BLOCKS)]
 
-        for o in range(PASSES):
+        def load_words(o):
             nc.sync.dma_start(word_table[o][:], x_words[o].rearrange("p n t -> p (n t)").bitcast(I32))
+
+        def load_h(b, o):
+            rows = hT[o * K_PASS : (o + 1) * K_PASS, b * P : (b + 1) * P]
+            nc.sync.dma_start(h_raw[b][o][:], rows.rearrange("(p j) m -> p j m", j=PACK))
+
+        load_words(0)
+        for q in range(QUADS):
+            nc.scalar.dma_start(
+                scale_table[:].bitcast(I32)[QUAD * q : QUAD * q + 4 * PASSES, :],
+                x_scales[:, 4 * q : 4 * q + 4, :].bitcast(I32),
+            )
+
         for b in range(BLOCKS):
-            for o in range(PASSES):
-                rows = hT[o * K_PASS : (o + 1) * K_PASS, b * P : (b + 1) * P]
-                nc.sync.dma_start(h_raw[b][o][:], rows.rearrange("(p j) m -> p j m", j=PACK))
+            load_h(b, 0)
+        load_words(1)
+        for b in range(BLOCKS):
+            load_h(b, 1)
         for g, g_sb in ((g1, g1_sb), (g2, g2_sb)):
             for b in range(BLOCKS):
                 nc.sync.dma_start(g_sb[b][:], g[b * P : (b + 1) * P, :])
 
-        x_scale = keep.tile([P, S], U8, name="x_scale", align_bytes=64)
-        nc.vector.tensor_copy(x_scale[:], scale_table[:].indirect(offsets[:]))
-        x_codes = [keep.tile([P, S], U32, name=f"x_codes{o}", align_bytes=64) for o in range(PASSES)]
-        for o in range(PASSES):
-            nc.vector.tensor_copy(x_codes[o][:], word_table[o][:].bitcast(U32).indirect(offsets[:]))
-
-        h_codes = [keep.tile([P, PASSES * P], U32, name=f"h_codes{b}", align_bytes=64) for b in range(BLOCKS)]
-        h_scale = [keep.tile([P, PASSES * P], U8, name=f"h_scale{b}", align_bytes=64) for b in range(BLOCKS)]
-        grouped = [keep.tile([P, PASSES, P, PACK], BF16, name=f"grouped{b}", align_bytes=64) for b in range(BLOCKS)]
         logits = [psum.tile([P, S], F32, name=f"logits{b}") for b in range(BLOCKS)]
 
-        def cast_h(b, o):
-            nc.scalar.activation(
-                grouped[b][:, o].rearrange("p (c i) j -> p c j i", i=4),
-                h_raw[b][o][:].rearrange("p j (c i) -> p c j i", i=4),
-                ACT.Copy,
-            )
+        def gather_words(o, tag):
+            codes = keep.tile([P, S], U32, name=f"x_codes{o}", tag=tag, align_bytes=64)
+            nc.vector.tensor_copy(codes[:], word_table[o][:].bitcast(U32).indirect(offsets[:]))
+            return codes
 
-        def quantize_h(b, o0, o1):
+        def multiply(o, blocks, x_codes, grouped_tag, codes_tag):
+            width = len(blocks) * P
+            grouped = keep.tile([P, width, PACK], BF16, name=f"grouped{o}_{blocks[0]}", tag=grouped_tag, align_bytes=64)
+            for i, b in enumerate(blocks):
+                nc.scalar.activation(grouped[:, i * P : (i + 1) * P, :], h_raw[b][o][:].rearrange("p j m -> p m j"), ACT.Copy)
+            h_codes = keep.tile([P, width], U32, name=f"h_codes{o}_{blocks[0]}", tag=codes_tag, align_bytes=64)
+            h_scale = keep.tile([P, width], U8, name=f"h_scale{o}_{blocks[0]}", align_bytes=64)
             nc.vector.quantize_mx(
-                out=h_codes[b][:, o0 * P : o1 * P].bitcast(FP8X4),
-                scales=h_scale[b][:, o0 * P : o1 * P],
-                in_=grouped[b][:, o0:o1].rearrange("p o m j -> p (o m j)"),
+                out=h_codes[:].bitcast(FP8X4),
+                scales=h_scale[:],
+                in_=grouped[:].rearrange("p m j -> p (m j)"),
             )
+            return h_codes, h_scale
 
-        def product(b, o):
+        def product(o, b, i, x_codes, h_codes, h_scale):
             nc.tensor.matmul_mx(
                 out=logits[b][:],
-                lhsT=h_codes[b][:, o * P : (o + 1) * P].bitcast(FP8X4),
-                lhsT_scale=h_scale[b][:, o * P : (o + 1) * P],
-                rhs=x_codes[o][:].bitcast(FP8X4),
+                lhsT=h_codes[:, i * P : (i + 1) * P].bitcast(FP8X4),
+                lhsT_scale=h_scale[:, i * P : (i + 1) * P],
+                rhs=x_codes[:].bitcast(FP8X4),
                 rhs_scale=x_scale[4 * o :, :],
                 start=(o == 0),
                 stop=(o == PASSES - 1),
             )
 
-        def column(name, width=1):
+        x_codes0 = gather_words(0, "x_codes0")
+        x_scale = keep.tile([P, S], U8, name="x_scale", align_bytes=64)
+        nc.vector.tensor_copy(x_scale[:], scale_table[:].indirect(offsets[:]))
+        hq = multiply(0, (0, 1), x_codes0, "grouped_slot", "scale_slot")
+        for b in range(BLOCKS):
+            product(0, b, b, x_codes0, *hq)
+        x_codes1 = gather_words(1, "grouped_slot")
+        hq = multiply(1, (0,), x_codes1, "grouped1_0", "h_codes1_0")
+        product(1, 0, 0, x_codes1, *hq)
+        hq = multiply(1, (1,), x_codes1, "reused", "h_codes1_1")
+        product(1, 1, 0, x_codes1, *hq)
+
+        def per_block(name, width):
             return [keep.tile([P, width], F32, name=f"{name}{b}") for b in range(BLOCKS)]
 
-        neg_max, total, inv_total = column("neg_max"), column("total"), column("inv_total")
-        raw1, norm1, raw2, norm2 = column("raw1_", 2), column("norm1_", 2), column("raw2_"), column("norm2_")
-        e, u, v, res = column("e", S), column("u", S), column("v", S), column("res", S)
-
-        def softmax(b):
-            nc.vector.reduce_max(neg_max[b][:], logits[b][:], AX.X, negate=True)
-            nc.scalar.activation(e[b][:], logits[b][:], ACT.Exp, bias=neg_max[b][:], accum_out=total[b][:])
-
-        def mass1(b):
-            nc.vector.scalar_tensor_tensor(u[b][:], g1_sb[b][:], -1.0, e[b][:], ALU.add, ALU.mult, accum_out=raw1[b][:, 0:1])
-            nc.vector.reciprocal(inv_total[b][:], total[b][:])
-
-        def small1(b):
-            nc.vector.tensor_scalar(norm1[b][:], raw1[b][:], inv_total[b][:], None, ALU.mult)
-
-        def round1(b):
-            nc.vector.scalar_tensor_tensor(u[b][:], g1_sb[b][:], norm1[b][:, 0:1], e[b][:], ALU.subtract, ALU.mult)
-
-        def mass2(b):
-            nc.vector.scalar_tensor_tensor(v[b][:], g2_sb[b][:], -1.0, u[b][:], ALU.add, ALU.mult, accum_out=raw2[b][:])
-
-        def small2(b):
-            nc.vector.tensor_scalar(norm2[b][:], raw2[b][:], inv_total[b][:], None, ALU.mult)
-
-        def round2(b, c0, c1):
-            nc.vector.scalar_tensor_tensor(v[b][:, c0:c1], g2_sb[b][:, c0:c1], norm2[b][:], u[b][:, c0:c1], ALU.subtract, ALU.mult)
-            nc.scalar.activation(res[b][:, c0:c1], v[b][:, c0:c1], ACT.Ln, bias=0.01, scale=norm1[b][:, 1:2])
-            nc.sync.dma_start(out[b * P : (b + 1) * P, c0:c1], res[b][:, c0:c1])
+        neg_max = [
+            keep.tile([P, 1], F32, name="neg_max0", tag="reused", align_bytes=64),
+            keep.tile([P, 1], F32, name="neg_max1"),
+        ]
+        total, inv_total = per_block("total", 1), per_block("inv_total", 1)
+        raw1, n1, n2 = per_block("raw1_", 1), per_block("n1_", 1), per_block("n2_", 1)
+        e, p0, p1, p2, res = (per_block(name, S) for name in ("e", "p0_", "p1_", "p2_", "res"))
 
         for b in range(BLOCKS):
-            nc.vector.memset(raw1[b][:, 1:2], float(S))
-
-        for o in range(PASSES):
-            cast_h(0, o)
-            quantize_h(0, o, o + 1)
-            product(0, o)
-        for o in range(PASSES):
-            cast_h(1, o)
-        quantize_h(1, 0, PASSES)
-        for o in range(PASSES):
-            product(1, o)
-        softmax(0)
-        mass1(0)
-        softmax(1)
-        small1(0)
-        round1(0)
-        mass1(1)
-        mass2(0)
-        small1(1)
-        round1(1)
-        small2(0)
-        round2(0, 0, S)
-        mass2(1)
-        small2(1)
-        round2(1, 0, S // 2)
-        round2(1, S // 2, S)
+            nc.vector.reduce_max(neg_max[b][:], logits[b][:], AX.X, negate=True)
+            nc.scalar.activation(e[b][:], logits[b][:], ACT.Exp, bias=neg_max[b][:], accum_out=total[b][:])
+        for b in range(BLOCKS):
+            nc.vector.reciprocal(inv_total[b][:], total[b][:])
+            nc.vector.scalar_tensor_tensor(p1[b][:], g1_sb[b][:], -1.0, e[b][:], ALU.add, ALU.mult, accum_out=raw1[b][:])
+            nc.scalar.activation(p0[b][:], e[b][:], ACT.Copy, scale=inv_total[b][:])
+            nc.scalar.activation(n1[b][:], raw1[b][:], ACT.Copy, scale=inv_total[b][:])
+        for b in range(BLOCKS):
+            nc.vector.scalar_tensor_tensor(p1[b][:], g1_sb[b][:], n1[b][:], p0[b][:], ALU.subtract, ALU.mult)
+        for b in range(BLOCKS):
+            nc.vector.scalar_tensor_tensor(p2[b][:], g2_sb[b][:], -1.0, p1[b][:], ALU.add, ALU.mult, accum_out=n2[b][:])
+        for b in range(BLOCKS):
+            for c in range(2):
+                cols = slice(c * S // 2, (c + 1) * S // 2)
+                nc.vector.scalar_tensor_tensor(p2[b][:, cols], g2_sb[b][:, cols], n2[b][:], p1[b][:, cols], ALU.subtract, ALU.mult)
+                nc.scalar.activation(res[b][:, cols], p2[b][:, cols], ACT.Ln, bias=0.01, scale=float(S))
+                nc.sync.dma_start(out[b * P : (b + 1) * P, cols], res[b][:, cols])

@@ -32,7 +32,6 @@ def tile_picked_ysynth_two_p_kernel(tc, x_words, x_scales, hT, g1, g2, offs, out
         psum = ctx.enter_context(tc.psum_pool(name="psum", bufs=1))
 
         offsets = keep.tile([P, S // 16], U16, name="offsets")
-        nc.sync.dma_start(offsets[:], offs)
 
         scale_table = keep.tile([P, T], U8, name="scale_table", tag="scale_slot", align_bytes=64)
         nc.vector.memset(scale_table[:].bitcast(I32), 0)
@@ -50,8 +49,9 @@ def tile_picked_ysynth_two_p_kernel(tc, x_words, x_scales, hT, g1, g2, offs, out
             nc.sync.dma_start(h_raw[b][o][:], rows.rearrange("(p j) m -> p j m", j=PACK))
 
         load_words(0)
+        nc.sync.dma_start(offsets[:], offs)
         for q in range(QUADS):
-            nc.scalar.dma_start(
+            nc.sync.dma_start(
                 scale_table[:].bitcast(I32)[QUAD * q : QUAD * q + 4 * PASSES, :],
                 x_scales[:, 4 * q : 4 * q + 4, :].bitcast(I32),
             )
@@ -76,7 +76,9 @@ def tile_picked_ysynth_two_p_kernel(tc, x_words, x_scales, hT, g1, g2, offs, out
             width = len(blocks) * P
             grouped = keep.tile([P, width, PACK], BF16, name=f"grouped{o}_{blocks[0]}", tag=grouped_tag, align_bytes=64)
             for i, b in enumerate(blocks):
-                nc.scalar.activation(grouped[:, i * P : (i + 1) * P, :], h_raw[b][o][:].rearrange("p j m -> p m j"), ACT.Copy)
+                src = h_raw[b][o][:].rearrange("p j (c i) -> p c j i", i=4)
+                dst = grouped[:, i * P : (i + 1) * P, :].rearrange("p (c i) j -> p c j i", i=4)
+                nc.scalar.activation(dst, src, ACT.Copy)
             h_codes = keep.tile([P, width], U32, name=f"h_codes{o}_{blocks[0]}", tag=codes_tag, align_bytes=64)
             h_scale = keep.tile([P, width], U8, name=f"h_scale{o}_{blocks[0]}", align_bytes=64)
             nc.vector.quantize_mx(

from contextlib import ExitStack

import concourse.mybir as mybir

K, T, S, V = 1024, 1024, 512, 256
FLOPS = 2 * K * S * V

F32 = mybir.dt.float32
BF16 = mybir.dt.bfloat16
I32 = mybir.dt.int32
U32 = mybir.dt.uint32
U16 = mybir.dt.uint16
U8 = mybir.dt.uint8
FP8X4 = mybir.dt.float8_e4m3fn_x4
ALU = mybir.AluOpType
ACT = mybir.ActivationFunctionType
AX = mybir.AxisListType

P = 128
PACK = 4
K_PASS = P * PACK
PASSES = K // K_PASS
BLOCKS = V // P
QUADS = 4
QUAD = P // QUADS


def tile_picked_ysynth_two_p_kernel(tc, x_words, x_scales, hT, g1, g2, offs, out):
    nc = tc.nc
    with ExitStack() as ctx:
        keep = ctx.enter_context(tc.tile_pool(name="keep", bufs=1))
        psum = ctx.enter_context(tc.psum_pool(name="psum", bufs=1))

        offsets = keep.tile([P, S // 16], U16, name="offsets")

        scale_table = keep.tile([P, T], U8, name="scale_table", tag="scale_slot", align_bytes=64)
        nc.vector.memset(scale_table[:].bitcast(I32), 0)

        word_table = [keep.tile([P, T], I32, name=f"word_table{o}", align_bytes=64) for o in range(PASSES)]
        h_raw = [[keep.tile([P, PACK, P], F32, name=f"h_raw{b}_{o}") for o in range(PASSES)] for b in range(BLOCKS)]
        g1_sb = [keep.tile([P, S], F32, name=f"g1_sb{b}") for b in range(BLOCKS)]
        g2_sb = [keep.tile([P, S], F32, name=f"g2_sb{b}") for b in range(BLOCKS)]

        def load_words(o):
            nc.sync.dma_start(word_table[o][:], x_words[o].rearrange("p n t -> p (n t)").bitcast(I32))

        def load_h(b, o):
            rows = hT[o * K_PASS : (o + 1) * K_PASS, b * P : (b + 1) * P]
            nc.sync.dma_start(h_raw[b][o][:], rows.rearrange("(p j) m -> p j m", j=PACK))

        load_words(0)
        nc.sync.dma_start(offsets[:], offs)
        for q in range(QUADS):
            nc.sync.dma_start(
                scale_table[:].bitcast(I32)[QUAD * q : QUAD * q + 4 * PASSES, :],
                x_scales[:, 4 * q : 4 * q + 4, :].bitcast(I32),
            )

        for b in range(BLOCKS):
            load_h(b, 0)
        load_words(1)
        for b in range(BLOCKS):
            load_h(b, 1)
        for g, g_sb in ((g1, g1_sb), (g2, g2_sb)):
            for b in range(BLOCKS):
                nc.sync.dma_start(g_sb[b][:], g[b * P : (b + 1) * P, :])

        logits = [psum.tile([P, S], F32, name=f"logits{b}") for b in range(BLOCKS)]

        def gather_words(o, tag):
            codes = keep.tile([P, S], U32, name=f"x_codes{o}", tag=tag, align_bytes=64)
            nc.vector.tensor_copy(codes[:], word_table[o][:].bitcast(U32).indirect(offsets[:]))
            return codes

        def multiply(o, blocks, x_codes, grouped_tag, codes_tag):
            width = len(blocks) * P
            grouped = keep.tile([P, width, PACK], BF16, name=f"grouped{o}_{blocks[0]}", tag=grouped_tag, align_bytes=64)
            for i, b in enumerate(blocks):
                src = h_raw[b][o][:].rearrange("p j (c i) -> p c j i", i=4)
                dst = grouped[:, i * P : (i + 1) * P, :].rearrange("p (c i) j -> p c j i", i=4)
                nc.scalar.activation(dst, src, ACT.Copy)
            h_codes = keep.tile([P, width], U32, name=f"h_codes{o}_{blocks[0]}", tag=codes_tag, align_bytes=64)
            h_scale = keep.tile([P, width], U8, name=f"h_scale{o}_{blocks[0]}", align_bytes=64)
            nc.vector.quantize_mx(
                out=h_codes[:].bitcast(FP8X4),
                scales=h_scale[:],
                in_=grouped[:].rearrange("p m j -> p (m j)"),
            )
            return h_codes, h_scale

        def product(o, b, i, x_codes, h_codes, h_scale):
            nc.tensor.matmul_mx(
                out=logits[b][:],
                lhsT=h_codes[:, i * P : (i + 1) * P].bitcast(FP8X4),
                lhsT_scale=h_scale[:, i * P : (i + 1) * P],
                rhs=x_codes[:].bitcast(FP8X4),
                rhs_scale=x_scale[4 * o :, :],
                start=(o == 0),
                stop=(o == PASSES - 1),
            )

        x_codes0 = gather_words(0, "x_codes0")
        x_scale = keep.tile([P, S], U8, name="x_scale", align_bytes=64)
        nc.vector.tensor_copy(x_scale[:], scale_table[:].indirect(offsets[:]))
        hq = multiply(0, (0, 1), x_codes0, "grouped_slot", "scale_slot")
        for b in range(BLOCKS):
            product(0, b, b, x_codes0, *hq)
        x_codes1 = gather_words(1, "grouped_slot")
        hq = multiply(1, (0,), x_codes1, "grouped1_0", "h_codes1_0")
        product(1, 0, 0, x_codes1, *hq)
        hq = multiply(1, (1,), x_codes1, "reused", "h_codes1_1")
        product(1, 1, 0, x_codes1, *hq)

        def per_block(name, width):
            return [keep.tile([P, width], F32, name=f"{name}{b}") for b in range(BLOCKS)]

        neg_max = [
            keep.tile([P, 1], F32, name="neg_max0", tag="reused", align_bytes=64),
            keep.tile([P, 1], F32, name="neg_max1"),
        ]
        total, inv_total = per_block("total", 1), per_block("inv_total", 1)
        raw1, n1, n2 = per_block("raw1_", 1), per_block("n1_", 1), per_block("n2_", 1)
        e, p0, p1, p2, res = (per_block(name, S) for name in ("e", "p0_", "p1_", "p2_", "res"))

        for b in range(BLOCKS):
            nc.vector.reduce_max(neg_max[b][:], logits[b][:], AX.X, negate=True)
            nc.scalar.activation(e[b][:], logits[b][:], ACT.Exp, bias=neg_max[b][:], accum_out=total[b][:])
        for b in range(BLOCKS):
            nc.vector.reciprocal(inv_total[b][:], total[b][:])
            nc.vector.scalar_tensor_tensor(p1[b][:], g1_sb[b][:], -1.0, e[b][:], ALU.add, ALU.mult, accum_out=raw1[b][:])
            nc.scalar.activation(p0[b][:], e[b][:], ACT.Copy, scale=inv_total[b][:])
            nc.scalar.activation(n1[b][:], raw1[b][:], ACT.Copy, scale=inv_total[b][:])
        for b in range(BLOCKS):
            nc.vector.scalar_tensor_tensor(p1[b][:], g1_sb[b][:], n1[b][:], p0[b][:], ALU.subtract, ALU.mult)
        for b in range(BLOCKS):
            nc.vector.scalar_tensor_tensor(p2[b][:], g2_sb[b][:], -1.0, p1[b][:], ALU.add, ALU.mult, accum_out=n2[b][:])
        for b in range(BLOCKS):
            for c in range(2):
                cols = slice(c * S // 2, (c + 1) * S // 2)
                nc.vector.scalar_tensor_tensor(p2[b][:, cols], g2_sb[b][:, cols], n2[b][:], p1[b][:, cols], ALU.subtract, ALU.mult)
                nc.scalar.activation(res[b][:, cols], p2[b][:, cols], ACT.Ln, bias=0.01, scale=float(S))
                nc.sync.dma_start(out[b * P : (b + 1) * P, cols], res[b][:, cols])
